import numpy as np
import ml_dtypes


def mxq(x, axis, fmt="e4m3"):
    dtype, down = {"e4m3": (ml_dtypes.float8_e4m3fn, 7), "e5m2": (ml_dtypes.float8_e5m2, 14)}[fmt]
    v = np.moveaxis(np.asarray(x, np.float32).astype(ml_dtypes.bfloat16).astype(np.float64), axis, -1)
    blocks = v.reshape(v.shape[:-1] + (-1, 32))
    amax = np.abs(blocks).max(-1, keepdims=True)
    byte = np.maximum(np.where(amax > 0, np.frexp(amax)[1] - 1 + 127, 0) - down, 1)
    scale = np.exp2(byte - 127.0)
    codes = (blocks / scale).astype(np.float32).astype(dtype).astype(np.float64)
    return np.moveaxis((codes * scale).reshape(v.shape), -1, axis)


WIDE = False


def mx_kscale(k):
    if not WIDE:
        return np.ones(k)
    levels = np.array([10, -10, 5, -5, 0])
    if k % 512:
        return np.exp2(np.random.permutation(np.resize(levels, k // 32))).repeat(32)
    a = np.empty((k // 512, 16))
    for p in range(k // 512):
        a[p, :8] = np.random.permutation(np.resize(levels, 8))
        for g in range(8):
            far = levels[np.abs(levels - a[p, g]) >= 10]
            a[p, g + 8] = far[np.random.randint(len(far))]
    return np.exp2(a.ravel()).repeat(32)


def f64(x):
    return np.asarray(x).astype(np.float64)


def striped(idx):
    return np.tile(idx.reshape(-1, 16).T, (8, 1)).astype(np.uint16)


def unstriped(offs):
    return offs[:16].T.reshape(-1).astype(np.int64)


E2M1 = np.array([0.0, 0.5, 1.0, 1.5, 2.0, 3.0, 4.0, 6.0, -0.0, -0.5, -1.0, -1.5, -2.0, -3.0, -4.0, -6.0])


def pack_weight(w, fmt):
    k, n = w.shape
    w = f64(np.asarray(w, np.float32).astype(ml_dtypes.bfloat16)).reshape(k // 32, 32, n)
    amax = np.abs(w).max(1)
    if fmt == "e4m3":
        byte = np.frexp(amax)[1] - 1 + 127 - 7
    else:
        mant, ex = np.frexp(amax / 6.0)
        byte = np.where(mant > 0.5, ex, ex - 1) + 127
    byte = np.clip(np.where(amax > 0, byte, 1), 1, 254)
    scaled = (w * np.exp2(127.0 - byte)[:, None, :]).reshape(k, n).astype(np.float32)
    by_word = np.ascontiguousarray(scaled.reshape(k // 512, 128, 4, n).transpose(0, 1, 3, 2))
    if fmt == "e4m3":
        words = by_word.astype(ml_dtypes.float8_e4m3fn).view(np.uint8)
    else:
        c = by_word.astype(ml_dtypes.float4_e2m1fn).view(np.uint8) & 0xF
        words = (c[..., 0::2] | (c[..., 1::2] << 4)).reshape(k // 512, 128, 2 * n)
    return np.ascontiguousarray(words), np.ascontiguousarray(byte.astype(np.uint8).reshape(k // 512, 16, n))


def unpack_weight(words, scales, fmt):
    g, _, n = scales.shape
    words = np.ascontiguousarray(words).reshape(g, 128, n, -1)
    if fmt == "e4m3":
        vals = words.view(ml_dtypes.float8_e4m3fn).astype(np.float64)
    else:
        nib = np.empty((g, 128, n, 4), np.uint8)
        nib[..., 0::2] = words & 0xF
        nib[..., 1::2] = words >> 4
        vals = E2M1[nib]
    vals = vals * np.repeat(np.exp2(scales.astype(np.float64) - 127.0), 8, axis=1)[..., None]
    return vals.transpose(0, 1, 3, 2).reshape(g * 512, n)


def gelu(v):
    return 0.5 * v * (1.0 + np.tanh(np.sqrt(2.0 / np.pi) * (v + 0.044715 * v**3)))


K, T, S, H, T2, P = 1536, 2048, 512, 1024, 1024, 512


def setup_inputs():
    n = np.random.standard_normal
    s = mx_kscale(K)[:, None]
    u = mx_kscale(H)[:, None]
    d = {}
    d["tab_words"], d["tab_scales"] = pack_weight(n((K, T)) * s, "e4m3")
    d["offs"] = striped(np.random.permutation(T)[:S])
    d["w1"] = (n((K, H)) / K ** 0.5 / s * u.T).astype(np.float32)
    d["w4_words"], d["w4_scales"] = pack_weight(n((K, H)) / K ** 0.5 / s * u.T, "e2m1")
    d["w8_words"], d["w8_scales"] = pack_weight(n((K, H)) / K ** 0.5 / s * u.T, "e4m3")
    d["page0"] = (n((H, T2)) * u).astype(np.float32)
    d["wgs"] = np.exp(0.3 * n((128, S))).astype(np.float32)
    d["offs2"] = striped(np.random.permutation(T2)[:S])
    d["offs3"] = striped(np.random.permutation(T2)[:P])
    d["cap"] = (np.random.uniform(0.6, 1.8, H) * u[:, 0]).astype(np.float32)
    d["gain"] = (n(H) / H ** 0.5 / u[:, 0] ** 2).astype(np.float32)
    d["lim"] = (0.4 + 0.8 * n((T2, P))).astype(np.float32)
    d["slot"] = np.exp(0.4 * n(T2)).astype(np.float32)
    return d


def reference(tab_words, tab_scales, offs, w1, w4_words, w4_scales, w8_words, w8_scales,
              page0, wgs, offs2, offs3, cap, gain, lim, slot):
    v = unpack_weight(tab_words, tab_scales, "e4m3")[:, unstriped(offs)]
    h1 = mxq(f64(w1), 0, "e4m3").T @ v
    h2 = unpack_weight(w4_words, w4_scales, "e2m1").T @ v
    h3 = unpack_weight(w8_words, w8_scales, "e4m3").T @ v
    h = np.maximum(np.maximum(h1, h2), h3)
    page = f64(page0).copy()
    page[:, unstriped(offs2)] = np.tile(f64(wgs), (H // 128, 1)) * h
    x = np.minimum(np.abs(page[:, unstriped(offs3)]), f64(cap)[:, None]) * f64(gain)[:, None]
    e = mxq(page, 0, "e4m3").T @ mxq(x, 0, "e4m3")
    return np.minimum(e, f64(lim)) * f64(slot)[:, None]

from contextlib import ExitStack

import concourse.mybir as mybir
from concourse.masks import make_identity

K, T, S, H, T2, NX = 1536, 2048, 512, 1024, 1024, 512
FLOPS = 2 * (3 * K * H * S + H * T2 * NX)

F32 = mybir.dt.float32
BF16 = mybir.dt.bfloat16
I32 = mybir.dt.int32
U32 = mybir.dt.uint32
U16 = mybir.dt.uint16
U8 = mybir.dt.uint8
FP8X4 = mybir.dt.float8_e4m3fn_x4
FP4X4 = mybir.dt.float4_e2m1fn_x4
ALU = mybir.AluOpType
ACT = mybir.ActivationFunctionType

P = 128
PACK = 4
KPASS = P * PACK
NA = K // KPASS
NS = H // P
NB = H // KPASS
RUN = 4
W1_CHUNKS = [(0, 128), (128, 256), (256, 512), (512, 768), (768, 1024)]
W8_CHUNKS = [(0, 128), (128, 512), (512, 1024)]
W4_CHUNKS = [(0, 256), (256, 1024)]
PIECE = 256


def chunk_of(chunks, col):
    return [n for n, (lo, hi) in enumerate(chunks) if lo <= col < hi][0]


def tile_list_hull_fouling_readout_kernel(
    tc, tab_words, tab_scales, offs, w1, w4_words, w4_scales, w8_words, w8_scales,
    page0, wgs, offs2, offs3, cap, gain, lim, slot, out,
):
    nc = tc.nc
    with ExitStack() as ctx:
        keep = ctx.enter_context(tc.tile_pool(name="keep", bufs=1))
        ring = ctx.enter_context(tc.tile_pool(name="ring", bufs=2))
        psum = ctx.enter_context(tc.psum_pool(name="psum", bufs=1))

        list1 = keep.tile([P, S // 16], U16, name="list1")
        list2 = keep.tile([P, S // 16], U16, name="list2")
        list3 = keep.tile([P, NX // 16], U16, name="list3")

        tab_sc = keep.tile([P, NA, T], U8, name="tab_sc", align_bytes=64)
        w8_sc = keep.tile([P, NA, H], U8, name="w8_sc", align_bytes=64)
        w4_sc = keep.tile([P, NA, H], U8, name="w4_sc", align_bytes=64)
        for planes, source, queue in ((tab_sc, tab_scales, nc.gpsimd), (w8_sc, w8_scales, nc.scalar), (w4_sc, w4_scales, nc.gpsimd)):
            nc.vector.memset(planes[:].bitcast(I32), 0)
            for quad in range(4):
                queue.dma_start(
                    out=planes[32 * quad : 32 * quad + 4, :, :].bitcast(I32),
                    in_=source[:, 4 * quad : 4 * quad + 4, :].rearrange("a q t -> q a t").bitcast(I32),
                )

        tab_w = [keep.tile([P, T], U32, name="tab_w%d" % a) for a in range(NA)]
        pages = [keep.tile([P, T2], F32, name="page%d" % s) for s in range(NS)]
        w8_w = [keep.tile([P, NA, hi - lo], U32, name="w8_w%d" % lo, align_bytes=64) for lo, hi in W8_CHUNKS]
        w4_w = [keep.tile([P, NA, 2 * (hi - lo)], U8, name="w4_w%d" % lo, align_bytes=64) for lo, hi in W4_CHUNKS]
        w1_raw = {}

        def load_tab(a):
            nc.sync.dma_start(out=tab_w[a][:].bitcast(I32), in_=tab_words[a].rearrange("p t i -> p (t i)").bitcast(I32))

        def load_w1(n):
            lo, hi = W1_CHUNKS[n]
            w1_raw[n] = ring.tile([P, NA, PACK, hi - lo], F32, name="w1_raw%d" % n, tag="stream")
            for a in range(NA):
                nc.sync.dma_start(
                    out=w1_raw[n][:, a, :, :],
                    in_=w1[KPASS * a : KPASS * (a + 1), lo:hi].rearrange("(p j) c -> p j c", j=PACK),
                )

        def load_w8(n):
            lo, hi = W8_CHUNKS[n]
            nc.sync.dma_start(
                out=w8_w[n][:].bitcast(I32),
                in_=w8_words.rearrange("a p c i -> p a (c i)")[:, :, 4 * lo : 4 * hi].bitcast(I32),
            )

        def load_w4(n):
            lo, hi = W4_CHUNKS[n]
            nc.sync.dma_start(
                out=w4_w[n][:].bitcast(I32),
                in_=w4_words.rearrange("a p c -> p a c")[:, :, 2 * lo : 2 * hi].bitcast(I32),
            )

        def load_page(s):
            nc.sync.dma_start(out=pages[s][:], in_=page0[P * s : P * (s + 1), :])

        wgs_t = keep.tile([P, S], F32, name="wgs_t", tag="late", align_bytes=64)

        nc.sync.dma_start(list1[:], offs)
        load_tab(0)
        load_w1(0)
        load_tab(1)
        load_w8(0)
        load_w4(0)
        load_tab(2)
        nc.sync.dma_start(out=wgs_t[:], in_=wgs)
        load_page(0)
        nc.sync.dma_start(list2[:], offs2)
        load_w1(1)
        load_w8(1)
        nc.sync.dma_start(list3[:], offs3)
        load_page(1)

        rows = keep.tile([P, P], F32, name="rows")
        ident = keep.tile([P, P], F32, name="ident")
        cols = keep.tile([P, 3 * NS], F32, name="cols")
        nc.gpsimd.memset(rows[:], 0.0)
        for n, vec in enumerate((cap, gain, slot)):
            nc.gpsimd.dma_start(out=rows[NS * n : NS * (n + 1), :], in_=vec.rearrange("(s q) -> s q", q=P))
        make_identity(nc, ident[:])

        v_w = [keep.tile([P, S], U32, name="v_w%d" % a, align_bytes=64) for a in range(NA)]
        v_sc = [keep.tile([P, S], U8, name="v_sc%d" % a, align_bytes=64) for a in range(NA)]
        for a in range(NA):
            nc.vector.tensor_copy(out=v_sc[a][:], in_=tab_sc[:, a, :].indirect(list1[:]))
            nc.vector.tensor_copy(out=v_w[a][:], in_=tab_w[a][:].indirect(list1[:]))

        w1_q = {}

        def quantise_w1(s):
            n = chunk_of(W1_CHUNKS, P * s)
            lo = P * s - W1_CHUNKS[n][0]
            woven = keep.tile([P, NA * P * PACK], BF16, name="w1_woven", tag="duo%d" % (s % 2), align_bytes=64)
            nc.scalar.copy(
                out=woven[:].rearrange("p (a c i j) -> p a c j i", a=NA, i=RUN, j=PACK),
                in_=w1_raw[n][:, :, :, lo : lo + P].rearrange("p a j (c i) -> p a c j i", i=RUN),
            )
            codes = ring.tile([P, NA * P], U32, name="w1_codes", bufs=4, align_bytes=64)
            scales = ring.tile([P, NA * P], U8, name="w1_scales", bufs=4, align_bytes=64)
            nc.vector.quantize_mx(out=codes[:].bitcast(FP8X4), scales=scales[:], in_=woven[:])
            w1_q[s] = (codes, scales)

        def product(s, n, sides):
            bank = psum.tile([P, S], F32, name="h%d" % n, tag="bank%d" % (3 * (s % 2) + n))
            for a, (words, plane) in enumerate(sides):
                nc.tensor.matmul_mx(
                    out=bank[:], lhsT=words, lhsT_scale=plane,
                    rhs=v_w[a][:].bitcast(FP8X4), rhs_scale=v_sc[a][:],
                    start=(a == 0), stop=(a == NA - 1),
                )
            return bank

        def product_w8(s):
            n = chunk_of(W8_CHUNKS, P * s)
            lo = P * s - W8_CHUNKS[n][0]
            sides = [(w8_w[n][:, a, lo : lo + P].bitcast(FP8X4), w8_sc[:, a, P * s : P * (s + 1)]) for a in range(NA)]
            return product(s, 0, sides)

        def product_w4(s):
            n = chunk_of(W4_CHUNKS, P * s)
            lo = 2 * (P * s - W4_CHUNKS[n][0])
            sides = [(w4_w[n][:, a, lo : lo + 2 * P].bitcast(FP4X4), w4_sc[:, a, P * s : P * (s + 1)]) for a in range(NA)]
            return product(s, 1, sides)

        def product_w1(s):
            codes, scales = w1_q[s]
            sides = [(codes[:, P * a : P * (a + 1)].bitcast(FP8X4), scales[:, P * a : P * (a + 1)]) for a in range(NA)]
            return product(s, 2, sides)

        def given_products(s):
            h8 = product_w8(s)
            h4 = product_w4(s)
            h8_sb = keep.tile([P, S], F32, name="h8_sb", tag="one")
            nc.scalar.copy(out=h8_sb[:], in_=h8[:])
            return h8_sb, h4

        dealt = [keep.tile([P, PACK, T2 + NX], BF16, name="dealt%d" % b) for b in range(NB)]
        woven_p = [keep.tile([P, T2 * PACK], BF16, name="woven_p%d" % b, align_bytes=64) for b in range(NB)]
        woven_x = [keep.tile([P, NX * PACK], BF16, name="woven_x%d" % b, align_bytes=64) for b in range(NB)]
        rounded = {}
        sizes = {}

        def fetch(s):
            picked = keep.tile([P, NX], F32, name="picked", tag="one")
            nc.vector.tensor_copy(out=picked[:], in_=pages[s][:].indirect(list3[:]))
            sizes[s] = ring.tile([P, NX], F32, name="sizes")
            nc.scalar.activation(out=sizes[s][:], in_=picked[:], func=ACT.Abs)

        def round_page(s):
            rounded[s] = keep.tile([P, T2 + NX], BF16, name="rounded", tag="tri%d" % ((s + 1) % 3), align_bytes=64)
            nc.scalar.copy(out=rounded[s][:, :T2], in_=pages[s][:])

        def make_x(s):
            nc.vector.tensor_scalar(
                out=rounded[s][:, T2:], in0=sizes[s][:],
                scalar1=cols[:, s : s + 1], scalar2=cols[:, NS + s : NS + s + 1], op0=ALU.min, op1=ALU.mult,
            )

        def deal(s, engine, lo, hi):
            b, quad = divmod(s, PACK)
            for t in range(PACK):
                engine.dma_start(out=dealt[b][32 * quad : 32 * (quad + 1), t, lo:hi], in_=rounded[s][t:P:PACK, lo:hi])

        def weave(copy, target, b, lo, first, width):
            copy(
                out=target[:, PACK * first : PACK * (first + width)].rearrange("p (c i t) -> p c t i", i=RUN, t=PACK),
                in_=dealt[b][:, :, lo + first : lo + first + width].rearrange("p t (c i) -> p c t i", i=RUN),
            )

        later_loads = {
            0: [lambda: load_w1(2), lambda: load_w4(1), lambda: load_page(2)],
            1: [lambda: load_w1(3), lambda: load_page(3), lambda: load_w8(2)],
            2: [lambda: load_page(4), lambda: load_page(5)],
            3: [lambda: load_w1(4), lambda: load_page(6), lambda: load_page(7)],
        }
        early_weaves = [(woven_p[0], 0, c) for c in range(0, T2, PIECE)] + [(woven_x[0], T2, c) for c in range(0, NX, PIECE)]

        quantise_w1(0)
        h8_sb, h4 = given_products(0)
        h1 = product_w1(0)
        for s in range(NS):
            for load in later_loads.get(s, []):
                load()
            larger = keep.tile([P, S], F32, name="larger", tag="tri%d" % (s % 3), align_bytes=64)
            nc.vector.tensor_tensor(out=larger[:], in0=h4[:], in1=h8_sb[:], op=ALU.max)
            if s > 0:
                fetch(s - 1)
            if s + 1 < NS:
                h8_sb, h4 = given_products(s + 1)
            if 0 < s < NS - 1:
                quantise_w1(s + 1)
            largest = keep.tile([P, S], F32, name="largest", tag="duo%d" % ((s + 1) % 2) if s else "tri2", align_bytes=64)
            nc.vector.tensor_tensor(out=largest[:], in0=h1[:], in1=larger[:], op=ALU.max)
            if s == 0:
                turned = psum.tile([P, P], F32, name="turned", tag="bank2")
                nc.tensor.transpose(turned[:], rows[:], ident[:])
                nc.scalar.copy(out=cols[:], in_=turned[:, : 3 * NS])
            else:
                round_page(s - 1)
                make_x(s - 1)
                if s == NS - 1:
                    deal(s - 1, nc.sync, 0, T2)
                    deal(s - 1, nc.sync, T2, T2 + NX)
                else:
                    deal(s - 1, nc.gpsimd, 0, T2 + NX)
            nc.vector.tensor_tensor(out=pages[s][:].indirect(list2[:]), in0=largest[:], in1=wgs_t[:], op=ALU.mult)
            if s == 0:
                quantise_w1(1)
            if s + 1 < NS:
                h1 = product_w1(s + 1)
            if s > PACK:
                for target, lo, c in early_weaves[2 * (s - PACK - 1) : 2 * (s - PACK)]:
                    weave(nc.scalar.copy, target, 0, lo, c, PIECE)

        lims = []
        for half in range(2):
            lim_t = ring.tile([P, NS // 2, NX], F32, name="lim%d" % half, tag="stream")
            nc.sync.dma_start(
                out=lim_t[:], in_=lim[T2 // 2 * half : T2 // 2 * (half + 1), :].rearrange("(i p) j -> p i j", p=P)
            )
            lims.append(lim_t)

        last = NS - 1
        round_page(last)
        deal(last, nc.sync, 0, T2)
        fetch(last)
        make_x(last)
        deal(last, nc.sync, T2, T2 + NX)

        codes2 = [
            keep.tile([P, T2 + NX], U32, name="codes_first", tag="late", align_bytes=64),
            keep.tile([P, T2 + NX], U32, name="codes_second", align_bytes=64),
        ]
        scales2 = [keep.tile([P, T2 + NX], U8, name="scales2_%d" % b, align_bytes=64) for b in range(NB)]

        def quantise2(b, source, lo, first, width):
            cs = slice(lo + first, lo + first + width)
            nc.vector.quantize_mx(
                out=codes2[b][:, cs].bitcast(FP8X4), scales=scales2[b][:, cs],
                in_=source[:, PACK * first : PACK * (first + width)],
            )

        def score(bank, b, i):
            ms = slice(P * i, P * (i + 1))
            nc.tensor.matmul_mx(
                out=bank[:], lhsT=codes2[b][:, ms].bitcast(FP8X4), lhsT_scale=scales2[b][:, ms],
                rhs=codes2[b][:, T2:].bitcast(FP8X4), rhs_scale=scales2[b][:, T2:],
                start=(b == 0), stop=(b == NB - 1),
            )

        quantise2(0, woven_p[0], 0, 0, T2)
        quantise2(0, woven_x[0], T2, 0, NX)
        sums = [psum.tile([P, NX], F32, name="e%d" % i, tag="bank%d" % i) for i in range(NS)]
        for i in range(NS):
            score(sums[i], 0, i)

        weave(nc.vector.tensor_copy, woven_x[1], 1, T2, 0, NX)
        quantise2(1, woven_x[1], T2, 0, NX)
        for c in range(0, T2, PIECE):
            weave(nc.scalar.copy, woven_p[1], 1, 0, c, PIECE)
        for i in range(NS):
            if P * i % PIECE == 0:
                quantise2(1, woven_p[1], 0, P * i, PIECE)
            score(sums[i], 1, i)
            limited = ring.tile([P, NX], F32, name="limited", bufs=3)
            nc.vector.tensor_tensor(out=limited[:], in0=sums[i][:], in1=lims[i // 4][:, i % 4, :], op=ALU.min)
            result = ring.tile([P, NX], F32, name="result", bufs=4)
            nc.scalar.activation(out=result[:], in_=limited[:], func=ACT.Copy, scale=cols[:, 2 * NS + i : 2 * NS + i + 1])
            nc.sync.dma_start(out=out[P * i : P * (i + 1), :], in_=result[:])
